import numpy as np
import ml_dtypes


def mxq(x, axis, fmt="e4m3"):
    dtype, down = {"e4m3": (ml_dtypes.float8_e4m3fn, 7), "e5m2": (ml_dtypes.float8_e5m2, 14)}[fmt]
    v = np.moveaxis(np.asarray(x, np.float32).astype(ml_dtypes.bfloat16).astype(np.float64), axis, -1)
    blocks = v.reshape(v.shape[:-1] + (-1, 32))
    amax = np.abs(blocks).max(-1, keepdims=True)
    byte = np.maximum(np.where(amax > 0, np.frexp(amax)[1] - 1 + 127, 0) - down, 1)
    scale = np.exp2(byte - 127.0)
    codes = (blocks / scale).astype(np.float32).astype(dtype).astype(np.float64)
    return np.moveaxis((codes * scale).reshape(v.shape), -1, axis)


WIDE = False


def mx_kscale(k):
    if not WIDE:
        return np.ones(k)
    levels = np.array([30, -30])
    if k % 512:
        return np.exp2(np.random.permutation(np.resize(levels, k // 32))).repeat(32)
    a = np.empty((k // 512, 16))
    for p in range(k // 512):
        a[p, :8] = np.random.permutation(np.resize(levels, 8))
        for g in range(8):
            far = levels[np.abs(levels - a[p, g]) >= 10]
            a[p, g + 8] = far[np.random.randint(len(far))]
    return np.exp2(a.ravel()).repeat(32)


def f64(x):
    return np.asarray(x).astype(np.float64)


def striped(idx):
    return np.tile(np.asarray(idx).reshape(-1, 16).T, (8, 1)).astype(np.uint16)


def unstriped(offs):
    return offs[:16].T.reshape(-1).astype(np.int64)


E2M1 = np.array([0.0, 0.5, 1.0, 1.5, 2.0, 3.0, 4.0, 6.0, -0.0, -0.5, -1.0, -1.5, -2.0, -3.0, -4.0, -6.0])


def pack_weight(w, fmt):
    k, n = w.shape
    w = f64(np.asarray(w, np.float32).astype(ml_dtypes.bfloat16)).reshape(k // 32, 32, n)
    amax = np.abs(w).max(1)
    if fmt == "e4m3":
        byte = np.frexp(amax)[1] - 1 + 127 - 7
    else:
        mant, ex = np.frexp(amax / 6.0)
        byte = np.where(mant > 0.5, ex, ex - 1) + 127
    byte = np.clip(np.where(amax > 0, byte, 1), 1, 254)
    scaled = (w * np.exp2(127.0 - byte)[:, None, :]).reshape(k, n).astype(np.float32)
    by_word = np.ascontiguousarray(scaled.reshape(k // 512, 128, 4, n).transpose(0, 1, 3, 2))
    if fmt == "e4m3":
        words = by_word.astype(ml_dtypes.float8_e4m3fn).view(np.uint8)
    else:
        c = by_word.astype(ml_dtypes.float4_e2m1fn).view(np.uint8) & 0xF
        words = (c[..., 0::2] | (c[..., 1::2] << 4)).reshape(k // 512, 128, 2 * n)
    return np.ascontiguousarray(words), np.ascontiguousarray(byte.astype(np.uint8).reshape(k // 512, 16, n))


def unpack_weight(words, scales, fmt):
    g, _, n = scales.shape
    words = np.ascontiguousarray(words).reshape(g, 128, n, -1)
    if fmt == "e4m3":
        vals = words.view(ml_dtypes.float8_e4m3fn).astype(np.float64)
    else:
        nib = np.empty((g, 128, n, 4), np.uint8)
        nib[..., 0::2] = words & 0xF
        nib[..., 1::2] = words >> 4
        vals = E2M1[nib]
    vals = vals * np.repeat(np.exp2(scales.astype(np.float64) - 127.0), 8, axis=1)[..., None]
    return vals.transpose(0, 1, 3, 2).reshape(g * 512, n)


K, T, J, R, N, Z = 512, 512, 256, 512, 256, 512


def setup_inputs():
    n = np.random.standard_normal
    idx = np.random.permutation(T)[:J]
    idx2 = np.random.permutation(Z)[:J]
    fk = mx_kscale(K)
    fr = mx_kscale(R)
    xtp = pack_weight(n((K, T)) / fk[:, None], "e4m3")
    wp = pack_weight(n((K, R)) * 1 / np.sqrt(K) * fk[:, None], "e2m1")
    wbp = pack_weight(n((R, N)) * 1 / np.sqrt(R) / fr[:, None], "e2m1")
    return {
        "xt_words": xtp[0],
        "xt_scales": xtp[1],
        "w_words": wp[0],
        "w_scales": wp[1],
        "us": (np.random.uniform(0.5, 1.5, (1, R)) * fr).astype(np.float32),
        "wb_words": wbp[0],
        "wb_scales": wbp[1],
        "tz": (n((N, Z)) * 0.6).astype(np.float32),
        "rw": (np.random.uniform(0.5, 2.0, (1, J))).astype(np.float32),
        "offs": striped(idx),
        "offs2": striped(idx2),
    }


def reference(xt_words, xt_scales, w_words, w_scales, us, wb_words, wb_scales, tz, rw, offs, offs2):
    idx = unstriped(offs)
    idx2 = unstriped(offs2)
    xtu = unpack_weight(xt_words, xt_scales, "e4m3")
    wu = unpack_weight(w_words, w_scales, "e2m1")
    wbu = unpack_weight(wb_words, wb_scales, "e2m1")
    xtidxg = xtu[:, idx]
    a = xtidxg.T @ wu
    m1 = np.max(a, axis=1, keepdims=True)
    hr = np.maximum(a, 0.0) / (m1 + 0.3) * f64(us)
    hid = hr.T
    hidq = mxq(hid, 0, "e5m2")
    p = wbu.T @ hidq
    y = np.maximum(p, f64(tz)[:, idx2]) * f64(rw)
    return y

@@ -1,0 +1,179 @@
+from contextlib import ExitStack
+
+import concourse.mybir as mybir
+from concourse.masks import make_identity
+
+K, T, J, R, N, Z = 512, 512, 256, 512, 256, 512
+FLOPS = 2 * K * J * R + 2 * R * N * J
+
+F32 = mybir.dt.float32
+BF16 = mybir.dt.bfloat16
+I32 = mybir.dt.int32
+U32 = mybir.dt.uint32
+U16 = mybir.dt.uint16
+U8 = mybir.dt.uint8
+E4M3 = mybir.dt.float8_e4m3fn_x4
+E5M2 = mybir.dt.float8_e5m2_x4
+E2M1 = mybir.dt.float4_e2m1fn_x4
+ALU = mybir.AluOpType
+ACT = mybir.ActivationFunctionType
+
+P = 128
+HALF = R // 2
+SLOT_TILES = J // P
+OUT_TILES = N // P
+
+
+def load_scales(queue, plane, scales, quads=range(4)):
+    rows = scales[0].bitcast(I32)
+    for q in quads:
+        src = rows[4 * q : 4 * q + 4, :]
+        queue.dma_start(plane[32 * q : 32 * q + 32, :].bitcast(I32), src.unsqueeze(0).to_broadcast([8, 4, rows.shape[1]]))
+
+
+def tile_list_rows_picked_peak_floored_kernel(
+    tc, xt_words, xt_scales, w_words, w_scales, us, wb_words, wb_scales, tz, rw, offs, offs2, out
+):
+    nc = tc.nc
+    with ExitStack() as ctx:
+        sb = ctx.enter_context(tc.tile_pool(name="sb", bufs=1))
+        ps = ctx.enter_context(tc.psum_pool(name="ps", bufs=1))
+
+        offsets = sb.tile([P, J // 16], U16, name="offsets")
+        offsets2 = sb.tile([P, J // 16], U16, name="offsets2")
+        x_words = sb.tile([P, T], I32, name="x_words", align_bytes=64)
+        x_bytes = sb.tile([P, T], U8, name="x_bytes", align_bytes=64)
+        w_codes = sb.tile([P, 2 * R], U8, name="w_codes", align_bytes=64)
+        w_bytes = sb.tile([P, R], U8, name="w_bytes", align_bytes=64)
+        wb_codes = sb.tile([P, 2 * N], U8, name="wb_codes", align_bytes=64)
+        wb_bytes = sb.tile([P, N], U8, name="wb_bytes", align_bytes=64)
+        us_cols = sb.tile([P, 4], F32, name="us_cols")
+        rw_cols = sb.tile([P, 2], F32, name="rw_cols")
+        tz_rows = sb.tile([P, OUT_TILES, Z], F32, name="tz_rows", align_bytes=64)
+        identity = sb.tile([P, P], F32, name="identity")
+
+        nc.sync.dma_start(offsets[:], offs)
+        load_scales(nc.sync, x_bytes, xt_scales)
+        nc.scalar.dma_start(x_words[:], xt_words[0].rearrange("p t b -> p (t b)").bitcast(I32))
+        nc.scalar.dma_start(w_codes[:].bitcast(I32), w_words[0].bitcast(I32))
+        load_scales(nc.sync, w_bytes, w_scales)
+        make_identity(nc, identity[:])
+        nc.gpsimd.dma_start(us_cols[:], us[0].rearrange("(p t) -> p t", t=4))
+        nc.gpsimd.dma_start(rw_cols[:], rw[0].rearrange("(p e) -> p e", e=2))
+        nc.sync.dma_start(offsets2[:], offs2)
+        nc.sync.dma_start(tz_rows[:], tz.rearrange("(m p) z -> p m z", p=P))
+        nc.sync.dma_start(wb_codes[:].bitcast(I32), wb_words[0].bitcast(I32))
+        load_scales(nc.sync, wb_bytes, wb_scales)
+
+        picked_bytes = sb.tile([P, J], U8, name="picked_bytes", align_bytes=64)
+        nc.vector.tensor_copy(picked_bytes[:], x_bytes[:].indirect(offsets[:]))
+        picked_words = []
+        for s in range(SLOT_TILES):
+            words = sb.tile([P, P], U32, name="picked_words%d" % s, align_bytes=64)
+            nc.vector.tensor_copy(words[:], x_words[:].bitcast(U32).indirect(offsets[:, 8 * s : 8 * s + 8]))
+            picked_words.append(words)
+
+        a_banks = {}
+        for s in range(SLOT_TILES):
+            for h in range(2):
+                bank = ps.tile([P, HALF], F32, name="a%d%d" % (s, h), tag="acc%d%d" % (s, h))
+                nc.tensor.matmul_mx(
+                    out=bank[:],
+                    lhsT=picked_words[s][:].bitcast(E4M3),
+                    lhsT_scale=picked_bytes[:, P * s : P * (s + 1)],
+                    rhs=w_codes[:, 2 * HALF * h : 2 * HALF * (h + 1)].bitcast(E2M1),
+                    rhs_scale=w_bytes[:, HALF * h : HALF * (h + 1)],
+                    start=True,
+                    stop=True,
+                )
+                a_banks[s, h] = bank
+
+        us_wide = ps.tile([P, 4, P], F32, name="us_wide")
+        for t in range(4):
+            nc.tensor.transpose(us_wide[:, t, :], us_cols[:, t : t + 1].to_broadcast([P, P]), identity[:])
+        rw_wide = ps.tile([P, 2, P], F32, name="rw_wide")
+        for e in range(2):
+            nc.tensor.transpose(rw_wide[:, e, :], rw_cols[:, e : e + 1].to_broadcast([P, P]), identity[:])
+
+        floor = sb.tile([P, OUT_TILES, J], F32, name="floor")
+        for m in range(OUT_TILES):
+            nc.scalar.activation(floor[:, m, :], tz_rows[:, m, :].indirect(offsets2[:]), ACT.Copy)
+
+        pos = [sb.tile([P, 2, P, 2], F32, name="pos%d" % s) for s in range(SLOT_TILES)]
+        peak = [[sb.tile([P, 1], F32, name="peak%d%d" % (s, h)) for h in range(2)] for s in range(SLOT_TILES)]
+        denom = [sb.tile([P, 1], F32, name="denom%d" % s) for s in range(SLOT_TILES)]
+        inv = [sb.tile([P, 1], F32, name="inv%d" % s) for s in range(SLOT_TILES)]
+        hid_rows = [[sb.tile([P, 2 * P], BF16, name="hid_rows%d%d" % (s, u), align_bytes=64) for u in range(2)] for s in range(SLOT_TILES)]
+
+        def rectify(s, h):
+            nc.vector.tensor_scalar(
+                pos[s][:, :, 64 * h : 64 * (h + 1), :],
+                a_banks[s, h][:].rearrange("j (p u e) -> j u p e", u=2, e=2),
+                0.0, 0.0, ALU.max, ALU.max, accum_out=peak[s][h][:],
+            )
+
+        def add_floor(s):
+            nc.vector.tensor_scalar(denom[s][:], peak[s][0][:], peak[s][1][:], 0.3, ALU.max, ALU.add)
+
+        def invert(s):
+            nc.vector.reciprocal(inv[s][:], denom[s][:])
+
+        def scale(s, u):
+            nc.vector.scalar_tensor_tensor(
+                hid_rows[s][u][:].rearrange("j (p e) -> j p e", e=2),
+                pos[s][:, u, :, :],
+                inv[s][:],
+                us_wide[:, 2 * u : 2 * u + 2, :].rearrange("j e p -> j p e"),
+                ALU.mult, ALU.mult,
+            )
+
+        rectify(0, 0)
+        rectify(0, 1)
+        rectify(1, 0)
+        add_floor(0)
+        rectify(1, 1)
+        invert(0)
+        add_floor(1)
+        scale(0, 0)
+        invert(1)
+        scale(0, 1)
+        scale(1, 0)
+        scale(1, 1)
+
+        for s in range(SLOT_TILES):
+            turned = ps.tile([P, 2, P], F32, name="turned%d" % s)
+            for u in range(2):
+                nc.tensor.transpose(turned[:, u, :], hid_rows[s][u][:].bitcast(F32), identity[:])
+            hid = sb.tile([P, 4 * P], BF16, name="hid%d" % s, align_bytes=64)
+            nc.scalar.copy(
+                hid[:].bitcast(F32).rearrange("p (j u) -> p j u", u=2), turned[:].rearrange("p u j -> p j u")
+            )
+            hid_codes = sb.tile([P, P], U32, name="hid_codes%d" % s, align_bytes=64)
+            hid_bytes = sb.tile([P, P], U8, name="hid_bytes%d" % s, align_bytes=64)
+            nc.vector.quantize_mx(out=hid_codes[:].bitcast(E5M2), scales=hid_bytes[:], in_=hid[:])
+            p_banks = []
+            for m in range(OUT_TILES):
+                bank = ps.tile([P, P], F32, name="p%d%d" % (s, m), tag="acc%d%d" % (s, m))
+                nc.tensor.matmul_mx(
+                    out=bank[:],
+                    lhsT=wb_codes[:, 2 * P * m : 2 * P * (m + 1)].bitcast(E2M1),
+                    lhsT_scale=wb_bytes[:, P * m : P * (m + 1)],
+                    rhs=hid_codes[:].bitcast(E5M2),
+                    rhs_scale=hid_bytes[:],
+                    start=True,
+                    stop=True,
+                )
+                p_banks.append(bank)
+            floored = [sb.tile([P, P], F32, name="floored%d%d" % (s, m)) for m in range(OUT_TILES)]
+            for m in range(OUT_TILES):
+                nc.vector.tensor_tensor(floored[m][:], p_banks[m][:], floor[:, m, P * s : P * (s + 1)], ALU.max)
+            for m in range(OUT_TILES):
+                y = sb.tile([P, P], F32, name="y%d%d" % (s, m))
+                nc.vector.tensor_tensor(
+                    y[:].rearrange("n (q e) -> n q e", e=2),
+                    floored[m][:].rearrange("n (q e) -> n q e", e=2),
+                    rw_wide[:, :, 64 * s : 64 * (s + 1)].rearrange("n e q -> n q e"),
+                    ALU.mult,
+                )
+                queue = nc.sync if m == 0 else nc.scalar
+                queue.dma_start(out[P * m : P * (m + 1), P * s : P * (s + 1)], y[:])

@@ -53,17 +53,22 @@ def tile_list_rows_picked_peak_floored_kernel(
         identity = sb.tile([P, P], F32, name="identity")
 
         nc.sync.dma_start(offsets[:], offs)
-        load_scales(nc.sync, x_bytes, xt_scales)
+        load_scales(nc.scalar, x_bytes, xt_scales, [0])
+        load_scales(nc.sync, x_bytes, xt_scales, [1])
         nc.scalar.dma_start(x_words[:], xt_words[0].rearrange("p t b -> p (t b)").bitcast(I32))
+        load_scales(nc.sync, x_bytes, xt_scales, [2])
         nc.scalar.dma_start(w_codes[:].bitcast(I32), w_words[0].bitcast(I32))
+        load_scales(nc.sync, x_bytes, xt_scales, [3])
         load_scales(nc.sync, w_bytes, w_scales)
-        make_identity(nc, identity[:])
-        nc.gpsimd.dma_start(us_cols[:], us[0].rearrange("(p t) -> p t", t=4))
-        nc.gpsimd.dma_start(rw_cols[:], rw[0].rearrange("(p e) -> p e", e=2))
+        nc.sync.dma_start(us_cols[:], us[0].rearrange("(p t) -> p t", t=4))
         nc.sync.dma_start(offsets2[:], offs2)
         nc.sync.dma_start(tz_rows[:], tz.rearrange("(m p) z -> p m z", p=P))
+        nc.sync.dma_start(rw_cols[:], rw[0].rearrange("(p e) -> p e", e=2))
         nc.sync.dma_start(wb_codes[:].bitcast(I32), wb_words[0].bitcast(I32))
         load_scales(nc.sync, wb_bytes, wb_scales)
+        make_identity(nc, identity[:])
+        warm = sb.tile([P, 1], F32, name="warm")
+        nc.scalar.activation(warm[:], identity[:, 0:1], ACT.Copy)
 
         picked_bytes = sb.tile([P, J], U8, name="picked_bytes", align_bytes=64)
         nc.vector.tensor_copy(picked_bytes[:], x_bytes[:].indirect(offsets[:]))

@@ -52,28 +52,32 @@ def tile_list_rows_picked_peak_floored_kernel(
         tz_rows = sb.tile([P, OUT_TILES, Z], F32, name="tz_rows", align_bytes=64)
         identity = sb.tile([P, P], F32, name="identity")
 
+        w_rows = w_scales[0].bitcast(I32)
+        nc.gpsimd.dma_start(w_bytes[0:84, :].bitcast(I32), w_rows[0:14, :].unsqueeze(0).to_broadcast([6, 14, R // 4]))
         nc.sync.dma_start(offsets[:], offs)
-        load_scales(nc.scalar, x_bytes, xt_scales, [0])
-        load_scales(nc.sync, x_bytes, xt_scales, [1])
         nc.scalar.dma_start(x_words[:], xt_words[0].rearrange("p t b -> p (t b)").bitcast(I32))
+        load_scales(nc.sync, x_bytes, xt_scales, [0])
+        load_scales(nc.scalar, x_bytes, xt_scales, [1])
         load_scales(nc.sync, x_bytes, xt_scales, [2])
         nc.scalar.dma_start(w_codes[:].bitcast(I32), w_words[0].bitcast(I32))
         load_scales(nc.sync, x_bytes, xt_scales, [3])
-        load_scales(nc.sync, w_bytes, w_scales)
+        nc.scalar.dma_start(w_bytes[84:128, :].bitcast(I32), w_rows[12:16, :].unsqueeze(0).to_broadcast([11, 4, R // 4]))
         nc.sync.dma_start(us_cols[:], us[0].rearrange("(p t) -> p t", t=4))
         nc.sync.dma_start(offsets2[:], offs2)
-        nc.sync.dma_start(tz_rows[:], tz.rearrange("(m p) z -> p m z", p=P))
         nc.sync.dma_start(rw_cols[:], rw[0].rearrange("(p e) -> p e", e=2))
+        nc.sync.dma_start(tz_rows[:], tz.rearrange("(m p) z -> p m z", p=P))
         nc.sync.dma_start(wb_codes[:].bitcast(I32), wb_words[0].bitcast(I32))
         load_scales(nc.sync, wb_bytes, wb_scales)
         make_identity(nc, identity[:])
         warm = sb.tile([P, 1], F32, name="warm")
-        nc.scalar.activation(warm[:], identity[:, 0:1], ACT.Copy)
+        warm_in = sb.tile([P, 1], F32, name="warm_in")
+        nc.vector.memset(warm_in[:], 0.0)
+        nc.scalar.activation(warm[:], warm_in[:], ACT.Copy)
 
         picked_bytes = sb.tile([P, J], U8, name="picked_bytes", align_bytes=64)
-        nc.vector.tensor_copy(picked_bytes[:], x_bytes[:].indirect(offsets[:]))
         picked_words = []
         for s in range(SLOT_TILES):
+            nc.vector.tensor_copy(picked_bytes[:, P * s : P * (s + 1)], x_bytes[:].indirect(offsets[:, 8 * s : 8 * s + 8]))
             words = sb.tile([P, P], U32, name="picked_words%d" % s, align_bytes=64)
             nc.vector.tensor_copy(words[:], x_words[:].bitcast(U32).indirect(offsets[:, 8 * s : 8 * s + 8]))
             picked_words.append(words)
@@ -145,18 +149,22 @@ def tile_list_rows_picked_peak_floored_kernel(
         scale(1, 0)
         scale(1, 1)
 
+        hid = []
         for s in range(SLOT_TILES):
             turned = ps.tile([P, 2, P], F32, name="turned%d" % s)
             for u in range(2):
                 nc.tensor.transpose(turned[:, u, :], hid_rows[s][u][:].bitcast(F32), identity[:])
-            hid = sb.tile([P, 4 * P], BF16, name="hid%d" % s, align_bytes=64)
+            tile = sb.tile([P, 4 * P], BF16, name="hid%d" % s, tag="hid%d" % s, align_bytes=64)
             nc.scalar.copy(
-                hid[:].bitcast(F32).rearrange("p (j u) -> p j u", u=2), turned[:].rearrange("p u j -> p j u")
+                tile[:].bitcast(F32).rearrange("p (j u) -> p j u", u=2), turned[:].rearrange("p u j -> p j u")
             )
+            hid.append(tile)
+
+        p_banks = {}
+        for s in range(SLOT_TILES):
             hid_codes = sb.tile([P, P], U32, name="hid_codes%d" % s, align_bytes=64)
             hid_bytes = sb.tile([P, P], U8, name="hid_bytes%d" % s, align_bytes=64)
-            nc.vector.quantize_mx(out=hid_codes[:].bitcast(E5M2), scales=hid_bytes[:], in_=hid[:])
-            p_banks = []
+            nc.vector.quantize_mx(out=hid_codes[:].bitcast(E5M2), scales=hid_bytes[:], in_=hid[s][:])
             for m in range(OUT_TILES):
                 bank = ps.tile([P, P], F32, name="p%d%d" % (s, m), tag="acc%d%d" % (s, m))
                 nc.tensor.matmul_mx(
@@ -168,15 +176,17 @@ def tile_list_rows_picked_peak_floored_kernel(
                     start=True,
                     stop=True,
                 )
-                p_banks.append(bank)
-            floored = [sb.tile([P, P], F32, name="floored%d%d" % (s, m)) for m in range(OUT_TILES)]
+                p_banks[s, m] = bank
+
+        for s in range(SLOT_TILES):
+            floored = sb.tile([P, OUT_TILES, P], F32, name="floored%d" % s, tag="hid%d" % (1 - s), align_bytes=64)
             for m in range(OUT_TILES):
-                nc.vector.tensor_tensor(floored[m][:], p_banks[m][:], floor[:, m, P * s : P * (s + 1)], ALU.max)
+                nc.vector.tensor_tensor(floored[:, m, :], p_banks[s, m][:], floor[:, m, P * s : P * (s + 1)], ALU.max)
             for m in range(OUT_TILES):
                 y = sb.tile([P, P], F32, name="y%d%d" % (s, m))
                 nc.vector.tensor_tensor(
                     y[:].rearrange("n (q e) -> n q e", e=2),
-                    floored[m][:].rearrange("n (q e) -> n q e", e=2),
+                    floored[:, m, :].rearrange("n (q e) -> n q e", e=2),
                     rw_wide[:, :, 64 * s : 64 * (s + 1)].rearrange("n e q -> n q e"),
                     ALU.mult,
                 )

from contextlib import ExitStack

import concourse.mybir as mybir
from concourse.masks import make_identity

K, T, J, R, N, Z = 512, 512, 256, 512, 256, 512
FLOPS = 2 * K * J * R + 2 * R * N * J

F32 = mybir.dt.float32
BF16 = mybir.dt.bfloat16
I32 = mybir.dt.int32
U32 = mybir.dt.uint32
U16 = mybir.dt.uint16
U8 = mybir.dt.uint8
E4M3 = mybir.dt.float8_e4m3fn_x4
E5M2 = mybir.dt.float8_e5m2_x4
E2M1 = mybir.dt.float4_e2m1fn_x4
ALU = mybir.AluOpType
ACT = mybir.ActivationFunctionType

P = 128
HALF = R // 2
SLOT_TILES = J // P
OUT_TILES = N // P


def load_scales(queue, plane, scales, quads=range(4)):
    rows = scales[0].bitcast(I32)
    for q in quads:
        src = rows[4 * q : 4 * q + 4, :]
        queue.dma_start(plane[32 * q : 32 * q + 32, :].bitcast(I32), src.unsqueeze(0).to_broadcast([8, 4, rows.shape[1]]))


def tile_list_rows_picked_peak_floored_kernel(
    tc, xt_words, xt_scales, w_words, w_scales, us, wb_words, wb_scales, tz, rw, offs, offs2, out
):
    nc = tc.nc
    with ExitStack() as ctx:
        sb = ctx.enter_context(tc.tile_pool(name="sb", bufs=1))
        ps = ctx.enter_context(tc.psum_pool(name="ps", bufs=1))

        offsets = sb.tile([P, J // 16], U16, name="offsets")
        offsets2 = sb.tile([P, J // 16], U16, name="offsets2")
        x_words = sb.tile([P, T], I32, name="x_words", align_bytes=64)
        x_bytes = sb.tile([P, T], U8, name="x_bytes", align_bytes=64)
        w_codes = sb.tile([P, 2 * R], U8, name="w_codes", align_bytes=64)
        w_bytes = sb.tile([P, R], U8, name="w_bytes", align_bytes=64)
        wb_codes = sb.tile([P, 2 * N], U8, name="wb_codes", align_bytes=64)
        wb_bytes = sb.tile([P, N], U8, name="wb_bytes", align_bytes=64)
        us_cols = sb.tile([P, 4], F32, name="us_cols")
        rw_cols = sb.tile([P, 2], F32, name="rw_cols")
        tz_rows = sb.tile([P, OUT_TILES, Z], F32, name="tz_rows", align_bytes=64)
        identity = sb.tile([P, P], F32, name="identity")

        w_rows = w_scales[0].bitcast(I32)
        nc.gpsimd.dma_start(w_bytes[0:84, :].bitcast(I32), w_rows[0:14, :].unsqueeze(0).to_broadcast([6, 14, R // 4]))
        nc.sync.dma_start(offsets[:], offs)
        nc.scalar.dma_start(x_words[:], xt_words[0].rearrange("p t b -> p (t b)").bitcast(I32))
        load_scales(nc.sync, x_bytes, xt_scales, [0])
        load_scales(nc.scalar, x_bytes, xt_scales, [1])
        load_scales(nc.sync, x_bytes, xt_scales, [2])
        nc.scalar.dma_start(w_codes[:].bitcast(I32), w_words[0].bitcast(I32))
        load_scales(nc.sync, x_bytes, xt_scales, [3])
        nc.scalar.dma_start(w_bytes[84:128, :].bitcast(I32), w_rows[12:16, :].unsqueeze(0).to_broadcast([11, 4, R // 4]))
        nc.sync.dma_start(us_cols[:], us[0].rearrange("(p t) -> p t", t=4))
        nc.sync.dma_start(offsets2[:], offs2)
        nc.sync.dma_start(rw_cols[:], rw[0].rearrange("(p e) -> p e", e=2))
        nc.sync.dma_start(tz_rows[:], tz.rearrange("(m p) z -> p m z", p=P))
        nc.sync.dma_start(wb_codes[:].bitcast(I32), wb_words[0].bitcast(I32))
        load_scales(nc.sync, wb_bytes, wb_scales)
        make_identity(nc, identity[:])
        warm = sb.tile([P, 1], F32, name="warm")
        warm_in = sb.tile([P, 1], F32, name="warm_in")
        nc.vector.memset(warm_in[:], 0.0)
        nc.scalar.activation(warm[:], warm_in[:], ACT.Copy)

        picked_bytes = sb.tile([P, J], U8, name="picked_bytes", align_bytes=64)
        picked_words = []
        for s in range(SLOT_TILES):
            nc.vector.tensor_copy(picked_bytes[:, P * s : P * (s + 1)], x_bytes[:].indirect(offsets[:, 8 * s : 8 * s + 8]))
            words = sb.tile([P, P], U32, name="picked_words%d" % s, align_bytes=64)
            nc.vector.tensor_copy(words[:], x_words[:].bitcast(U32).indirect(offsets[:, 8 * s : 8 * s + 8]))
            picked_words.append(words)

        a_banks = {}
        for s in range(SLOT_TILES):
            for h in range(2):
                bank = ps.tile([P, HALF], F32, name="a%d%d" % (s, h), tag="acc%d%d" % (s, h))
                nc.tensor.matmul_mx(
                    out=bank[:],
                    lhsT=picked_words[s][:].bitcast(E4M3),
                    lhsT_scale=picked_bytes[:, P * s : P * (s + 1)],
                    rhs=w_codes[:, 2 * HALF * h : 2 * HALF * (h + 1)].bitcast(E2M1),
                    rhs_scale=w_bytes[:, HALF * h : HALF * (h + 1)],
                    start=True,
                    stop=True,
                )
                a_banks[s, h] = bank

        us_wide = ps.tile([P, 4, P], F32, name="us_wide")
        for t in range(4):
            nc.tensor.transpose(us_wide[:, t, :], us_cols[:, t : t + 1].to_broadcast([P, P]), identity[:])
        rw_wide = ps.tile([P, 2, P], F32, name="rw_wide")
        for e in range(2):
            nc.tensor.transpose(rw_wide[:, e, :], rw_cols[:, e : e + 1].to_broadcast([P, P]), identity[:])

        floor = sb.tile([P, OUT_TILES, J], F32, name="floor")
        for m in range(OUT_TILES):
            nc.scalar.activation(floor[:, m, :], tz_rows[:, m, :].indirect(offsets2[:]), ACT.Copy)

        pos = [sb.tile([P, 2, P, 2], F32, name="pos%d" % s) for s in range(SLOT_TILES)]
        peak = [[sb.tile([P, 1], F32, name="peak%d%d" % (s, h)) for h in range(2)] for s in range(SLOT_TILES)]
        denom = [sb.tile([P, 1], F32, name="denom%d" % s) for s in range(SLOT_TILES)]
        inv = [sb.tile([P, 1], F32, name="inv%d" % s) for s in range(SLOT_TILES)]
        hid_rows = [[sb.tile([P, 2 * P], BF16, name="hid_rows%d%d" % (s, u), align_bytes=64) for u in range(2)] for s in range(SLOT_TILES)]

        def rectify(s, h):
            nc.vector.tensor_scalar(
                pos[s][:, :, 64 * h : 64 * (h + 1), :],
                a_banks[s, h][:].rearrange("j (p u e) -> j u p e", u=2, e=2),
                0.0, 0.0, ALU.max, ALU.max, accum_out=peak[s][h][:],
            )

        def add_floor(s):
            nc.vector.tensor_scalar(denom[s][:], peak[s][0][:], peak[s][1][:], 0.3, ALU.max, ALU.add)

        def invert(s):
            nc.vector.reciprocal(inv[s][:], denom[s][:])

        def scale(s, u):
            nc.vector.scalar_tensor_tensor(
                hid_rows[s][u][:].rearrange("j (p e) -> j p e", e=2),
                pos[s][:, u, :, :],
                inv[s][:],
                us_wide[:, 2 * u : 2 * u + 2, :].rearrange("j e p -> j p e"),
                ALU.mult, ALU.mult,
            )

        rectify(0, 0)
        rectify(0, 1)
        rectify(1, 0)
        add_floor(0)
        rectify(1, 1)
        invert(0)
        add_floor(1)
        scale(0, 0)
        invert(1)
        scale(0, 1)
        scale(1, 0)
        scale(1, 1)

        hid = []
        for s in range(SLOT_TILES):
            turned = ps.tile([P, 2, P], F32, name="turned%d" % s)
            for u in range(2):
                nc.tensor.transpose(turned[:, u, :], hid_rows[s][u][:].bitcast(F32), identity[:])
            tile = sb.tile([P, 4 * P], BF16, name="hid%d" % s, tag="hid%d" % s, align_bytes=64)
            nc.scalar.copy(
                tile[:].bitcast(F32).rearrange("p (j u) -> p j u", u=2), turned[:].rearrange("p u j -> p j u")
            )
            hid.append(tile)

        p_banks = {}
        for s in range(SLOT_TILES):
            hid_codes = sb.tile([P, P], U32, name="hid_codes%d" % s, align_bytes=64)
            hid_bytes = sb.tile([P, P], U8, name="hid_bytes%d" % s, align_bytes=64)
            nc.vector.quantize_mx(out=hid_codes[:].bitcast(E5M2), scales=hid_bytes[:], in_=hid[s][:])
            for m in range(OUT_TILES):
                bank = ps.tile([P, P], F32, name="p%d%d" % (s, m), tag="acc%d%d" % (s, m))
                nc.tensor.matmul_mx(
                    out=bank[:],
                    lhsT=wb_codes[:, 2 * P * m : 2 * P * (m + 1)].bitcast(E2M1),
                    lhsT_scale=wb_bytes[:, P * m : P * (m + 1)],
                    rhs=hid_codes[:].bitcast(E5M2),
                    rhs_scale=hid_bytes[:],
                    start=True,
                    stop=True,
                )
                p_banks[s, m] = bank

        for s in range(SLOT_TILES):
            floored = sb.tile([P, OUT_TILES, P], F32, name="floored%d" % s, tag="hid%d" % (1 - s), align_bytes=64)
            for m in range(OUT_TILES):
                nc.vector.tensor_tensor(floored[:, m, :], p_banks[s, m][:], floor[:, m, P * s : P * (s + 1)], ALU.max)
            for m in range(OUT_TILES):
                y = sb.tile([P, P], F32, name="y%d%d" % (s, m))
                nc.vector.tensor_tensor(
                    y[:].rearrange("n (q e) -> n q e", e=2),
                    floored[:, m, :].rearrange("n (q e) -> n q e", e=2),
                    rw_wide[:, :, 64 * s : 64 * (s + 1)].rearrange("n e q -> n q e"),
                    ALU.mult,
                )
                queue = nc.sync if m == 0 else nc.scalar
                queue.dma_start(out[P * m : P * (m + 1), P * s : P * (s + 1)], y[:])
